import numpy as np
import ml_dtypes


def mxq(x, axis, fmt="e4m3"):
    dtype, down = {"e4m3": (ml_dtypes.float8_e4m3fn, 7), "e5m2": (ml_dtypes.float8_e5m2, 14)}[fmt]
    v = np.moveaxis(np.asarray(x, np.float32).astype(ml_dtypes.bfloat16).astype(np.float64), axis, -1)
    blocks = v.reshape(v.shape[:-1] + (-1, 32))
    amax = np.abs(blocks).max(-1, keepdims=True)
    byte = np.maximum(np.where(amax > 0, np.frexp(amax)[1] - 1 + 127, 0) - down, 1)
    scale = np.exp2(byte - 127.0)
    codes = (blocks / scale).astype(np.float32).astype(dtype).astype(np.float64)
    return np.moveaxis((codes * scale).reshape(v.shape), -1, axis)


WIDE = False


def mx_kscale(k):
    if not WIDE:
        return np.ones(k)
    levels = np.array([10, -10, 5, -5, 0])
    if k % 512:
        return np.exp2(np.random.permutation(np.resize(levels, k // 32))).repeat(32)
    a = np.empty((k // 512, 16))
    for p in range(k // 512):
        a[p, :8] = np.random.permutation(np.resize(levels, 8))
        for g in range(8):
            far = levels[np.abs(levels - a[p, g]) >= 10]
            a[p, g + 8] = far[np.random.randint(len(far))]
    return np.exp2(a.ravel()).repeat(32)


def f64(x):
    return np.asarray(x).astype(np.float64)


def striped(idx):
    return np.tile(idx.reshape(-1, 16).T, (8, 1)).astype(np.uint16)


def unstriped(offs):
    return offs[:16].T.reshape(-1).astype(np.int64)


def striped8(idx):
    return np.concatenate([x.reshape(-1, 16).T for x in idx]).astype(np.uint16)


def runs(offs, k):
    lists = np.stack([offs[16 * r : 16 * r + 16].T.reshape(-1) for r in range(8)]).astype(np.int64)
    return lists[np.arange(k) % 512 // 64]


def pack_weight(w):
    k, n = w.shape
    w = f64(np.asarray(w, np.float32).astype(ml_dtypes.bfloat16)).reshape(k // 32, 32, n)
    amax = np.abs(w).max(1)
    byte = np.clip(np.where(amax > 0, np.frexp(amax)[1] - 1 + 127 - 7, 1), 1, 254)
    scaled = (w * np.exp2(127.0 - byte)[:, None, :]).reshape(k, n).astype(np.float32)
    words = np.ascontiguousarray(scaled.reshape(k // 512, 128, 4, n).transpose(0, 1, 3, 2)).astype(ml_dtypes.float8_e4m3fn).view(np.uint8)
    return words, np.ascontiguousarray(byte.astype(np.uint8).reshape(k // 512, 16, n))


def unpack_weight(words, scales):
    g, p, n, _ = words.shape
    vals = np.ascontiguousarray(words).view(ml_dtypes.float8_e4m3fn).astype(np.float64) * np.repeat(np.exp2(scales.astype(np.float64) - 127.0), 8, axis=1)[..., None]
    return vals.transpose(0, 1, 3, 2).reshape(g * 512, n)


E2M1 = np.array([0.0, 0.5, 1.0, 1.5, 2.0, 3.0, 4.0, 6.0, -0.0, -0.5, -1.0, -1.5, -2.0, -3.0, -4.0, -6.0])


def pack_fp4(w):
    k, n = w.shape
    w = f64(np.asarray(w, np.float32).astype(ml_dtypes.bfloat16)).reshape(k // 32, 32, n)
    amax = np.abs(w).max(1)
    mant, ex = np.frexp(amax / 6.0)
    byte = np.clip(np.where(amax > 0, np.where(mant > 0.5, ex, ex - 1) + 127, 1), 1, 254)
    scaled = (w * np.exp2(127.0 - byte)[:, None, :]).reshape(k, n).astype(np.float32)
    c = np.ascontiguousarray(scaled.reshape(k // 512, 128, 4, n).transpose(0, 1, 3, 2)).astype(ml_dtypes.float4_e2m1fn).view(np.uint8) & 0xF
    words = (c[..., 0::2] | (c[..., 1::2] << 4)).reshape(k // 512, 128, 2 * n)
    return np.ascontiguousarray(words), np.ascontiguousarray(byte.astype(np.uint8).reshape(k // 512, 16, n))


def unpack_fp4(words, scales):
    g, _, n = scales.shape
    words = np.ascontiguousarray(words).reshape(g, 128, n, 2)
    nib = np.empty((g, 128, n, 4), np.uint8)
    nib[..., 0::2] = words & 0xF
    nib[..., 1::2] = words >> 4
    vals = E2M1[nib] * np.repeat(np.exp2(scales.astype(np.float64) - 127.0), 8, axis=1)[..., None]
    return vals.transpose(0, 1, 3, 2).reshape(g * 512, n)


def planes(y):
    n, m = y.shape
    v = y.astype(np.float32).astype(ml_dtypes.bfloat16).astype(np.float64).reshape(n // 32, 32, m)
    top = np.abs(v).max(1)
    byte = np.clip(np.where(top > 0, np.frexp(top)[1] - 1 + 127 - 7, 1), 1, 254)
    codes = (v * np.exp2(127.0 - byte)[:, None, :]).reshape(n, m).astype(np.float32).astype(ml_dtypes.float8_e4m3fn).view(np.uint8)
    words = codes.reshape(n // 512, 128, 4, m).transpose(0, 1, 3, 2)
    return np.ascontiguousarray(words), np.ascontiguousarray(byte.astype(np.uint8).reshape(n // 512, 16, m))


K, T, S, N, G, H, W = 512, 2048, 256, 512, 2048, 512, 1024


def setup_inputs():
    n = np.random.standard_normal
    s = mx_kscale(K)[:, None]
    u = mx_kscale(K)
    packed_xT = pack_weight(n((K, T)) * s)
    packed_dT = pack_weight(n((K, G)) / s)
    packed_w1 = pack_fp4(n((H, N)) / np.sqrt(H) / u[:, None])
    return {
        "x_words": packed_xT[0],
        "x_scales": packed_xT[1],
        "d_words": packed_dT[0],
        "d_scales": packed_dT[1],
        "gn": (np.random.uniform(0.5, 1.5, (H, 1)) * u[:, None]).astype(np.float32),
        "w1_words": packed_w1[0],
        "w1_scales": packed_w1[1],
        "offs": striped(np.random.permutation(T)[:S]),
        "k1": striped8(np.random.randint(0, G, (8, H))),
        "n1": striped(np.random.randint(0, S, W)),
        "n2": striped(np.random.randint(0, S, W)),
    }


def reference(x_words, x_scales, d_words, d_scales, gn, w1_words, w1_scales, offs, k1, n1, n2):
    d_k1 = unpack_weight(d_words, d_scales)[np.arange(K)[:, None], runs(k1, K)]
    xq = unpack_weight(x_words, x_scales)[:, unstriped(offs)]
    h = 0.0625 * (d_k1.T @ xq)
    mb = h[:, unstriped(n1)]
    mx = mb.reshape(H, S, 4).max(axis=2)
    z = f64(gn) * (h - mx)
    h2 = unpack_fp4(w1_words, w1_scales).T @ mxq(z, 0, "e4m3")
    mb2 = h2[:, unstriped(n2)]
    mx2 = mb2.reshape(N, S, 4).max(axis=2)
    mn = mb2.reshape(N, S, 4).min(axis=2)
    out_0 = mx2 * np.tanh(h2 - mn)
    return (out_0,) + planes(out_0)

@@ -1,0 +1,272 @@
+from contextlib import ExitStack
+
+import concourse.mybir as mybir
+
+F32 = mybir.dt.float32
+BF16 = mybir.dt.bfloat16
+I32 = mybir.dt.int32
+U32 = mybir.dt.uint32
+U16 = mybir.dt.uint16
+U8 = mybir.dt.uint8
+FP8X4 = mybir.dt.float8_e4m3fn_x4
+FP4X4 = mybir.dt.float4_e2m1fn_x4
+ALU = mybir.AluOpType
+ACT = mybir.ActivationFunctionType
+AXIS = mybir.AxisListType
+
+P = 128
+PACK = 4
+TABLE = 2048
+S = 256
+H = 512
+MEMBERS = 4
+HALF = S // 2
+QCOLS = 64
+PIECES_1 = (128, 64, 64)
+PIECES_2 = (64, 64, 64, 32, 32)
+SPARE = 16
+
+FLOPS = 2 * 2 * 512 * 512 * 256
+
+
+def starts(widths):
+    return [(sum(widths[:i]), w) for i, w in enumerate(widths)]
+
+
+def tile_picked_pqlaygmaxdgtan_none_po_kernel(
+    tc, x_words, x_scales, d_words, d_scales, gn, w1_words, w1_scales, offs, k1, n1, n2, out_0, out_1, out_2
+):
+    nc = tc.nc
+    with ExitStack() as ctx:
+        keep = ctx.enter_context(tc.tile_pool(name="keep", bufs=1))
+        ring = ctx.enter_context(tc.tile_pool(name="ring", bufs=3))
+        psum = ctx.enter_context(tc.psum_pool(name="psum", bufs=1))
+
+        k1_t = keep.tile([P, H // 16], U16, name="k1_t")
+        offs_t = keep.tile([P, S // 16], U16, name="offs_t")
+        n1_t = keep.tile([P, MEMBERS * S // 16], U16, name="n1_t")
+        n2_t = keep.tile([P, MEMBERS * S // 16], U16, name="n2_t")
+
+        d_bytes = keep.tile([P, TABLE], U8, name="d_bytes")
+        x_bytes = keep.tile([P, TABLE], U8, name="x_bytes")
+        planes_1 = keep.tile([P, H + S], U8, name="planes_1", align_bytes=64)
+        nc.vector.memset(d_bytes[:].bitcast(I32), 0)
+        nc.vector.memset(x_bytes[:].bitcast(I32), 0)
+        nc.vector.memset(planes_1[:].bitcast(I32), 0)
+
+        d_table = keep.tile([P, TABLE], U32, name="d_table")
+        x_table = keep.tile([P, TABLE], U32, name="x_table")
+        gain = keep.tile([P, PACK], F32, name="gain")
+        nc.sync.dma_start(k1_t[:], k1)
+        nc.sync.dma_start(offs_t[:], offs)
+        nc.sync.dma_start(n1_t[:], n1)
+        nc.sync.dma_start(n2_t[:], n2)
+        nc.sync.dma_start(gain[:], gn.rearrange("(p t) o -> p (t o)", t=PACK))
+        nc.scalar.dma_start(d_bytes[0:P:8, :].bitcast(I32), d_scales[0].bitcast(I32))
+        nc.scalar.dma_start(x_bytes[0:P:8, :].bitcast(I32), x_scales[0].bitcast(I32))
+        nc.sync.dma_start(d_table[:].bitcast(I32), d_words[0].rearrange("p n t -> p (n t)").bitcast(I32))
+        nc.sync.dma_start(x_table[:].bitcast(I32), x_words[0].rearrange("p n t -> p (n t)").bitcast(I32))
+
+        wide_1 = MEMBERS * max(PIECES_1) + SPARE
+        wide_2 = MEMBERS * max(PIECES_2) + SPARE
+        h_rows = [keep.tile([P, wide_1], F32, name="h_rows%d" % t) for t in range(PACK)]
+        h2_rows = [keep.tile([P, wide_2], F32, name="h2_rows%d" % t) for t in range(PACK)]
+        for t in range(PACK):
+            nc.vector.memset(h_rows[t][:, S:], 0.0)
+            nc.vector.memset(h2_rows[t][:, S:], 0.0)
+
+        neg_gain = keep.tile([P, PACK], F32, name="neg_gain")
+        nc.scalar.activation(neg_gain[:], gain[:], ACT.Copy, scale=-1.0)
+
+        d_bytes_picked = keep.tile([P, H], U8, name="d_bytes_picked")
+        x_bytes_picked = keep.tile([P, S], U8, name="x_bytes_picked")
+        staged = keep.tile([P, H + S], U8, name="staged", tag="staged", align_bytes=64)
+        nc.vector.tensor_copy(d_bytes_picked[:], d_bytes[:].indirect(k1_t[:]))
+        nc.vector.tensor_copy(x_bytes_picked[:], x_bytes[:].indirect(offs_t[:]))
+        nc.vector.tensor_copy(
+            staged[:, :H].rearrange("p (t m) -> p t m", t=PACK),
+            d_bytes_picked[:].rearrange("p (m t) -> p t m", t=PACK),
+        )
+        nc.vector.tensor_copy(staged[:, H:], x_bytes_picked[:])
+        for r in range(4):
+            nc.sync.dma_start(planes_1[r:P:32, :].bitcast(I32), staged[8 * r : P : 32, :].bitcast(I32))
+
+        d_picked = keep.tile([P, H], U32, name="d_picked")
+        d_codes = keep.tile([P, H], U32, name="d_codes", align_bytes=64)
+        x_codes = keep.tile([P, S], U32, name="x_codes", align_bytes=64)
+        nc.vector.tensor_copy(d_picked[:], d_table[:].indirect(k1_t[:]))
+        nc.vector.tensor_copy(
+            d_codes[:].bitcast(I32).rearrange("p (t m) -> p t m", t=PACK),
+            d_picked[:].bitcast(I32).rearrange("p (m t) -> p t m", t=PACK),
+        )
+        nc.vector.tensor_copy(x_codes[:], x_table[:].indirect(offs_t[:]))
+
+        gained = keep.tile([P, PACK, S], F32, name="gained")
+        for t in range(PACK):
+            acc = psum.tile([P, S], F32, name="h_acc%d" % t)
+            nc.tensor.matmul_mx(
+                acc[:],
+                lhsT=d_codes[:, t * P : (t + 1) * P].bitcast(FP8X4),
+                lhsT_scale=planes_1[:, t * P : (t + 1) * P],
+                rhs=x_codes[:].bitcast(FP8X4),
+                rhs_scale=planes_1[:, H:],
+                start=True,
+                stop=True,
+            )
+            if t == 0:
+                nc.scalar.activation(h_rows[t][:, :S], acc[:], ACT.Copy, scale=0.0625)
+            else:
+                nc.vector.tensor_scalar(h_rows[t][:, :S], acc[:], 0.0625, None, ALU.mult)
+        for t in range(PACK):
+            nc.vector.tensor_scalar(gained[:, t, :], h_rows[t][:, :S], gain[:, t : t + 1], None, ALU.mult)
+
+        w_raw = keep.tile([P, 2 * H], U8, name="w_raw", tag="staged", align_bytes=64)
+        w_bytes = keep.tile([P, H], U8, name="w_bytes", tag="d_bytes_picked")
+        w_codes = keep.tile([P, 2 * H], U8, name="w_codes", align_bytes=64)
+        w_plane = keep.tile([P, H], U8, name="w_plane", align_bytes=64)
+        nc.sync.dma_start(w_raw[:].bitcast(I32), w1_words[0].bitcast(I32))
+        nc.vector.memset(w_bytes[:].bitcast(I32), 0)
+        for q in range(4):
+            nc.sync.dma_start(w_bytes[32 * q : 32 * q + 4, :].bitcast(I32), w1_scales[0, 4 * q : 4 * q + 4, :].bitcast(I32))
+
+        def deal_w1():
+            nc.vector.tensor_copy(
+                w_codes[:].rearrange("p (t m b) -> p t m b", t=PACK, b=2),
+                w_raw[:].rearrange("p (m t b) -> p t m b", t=PACK, b=2),
+            )
+            nc.vector.tensor_copy(
+                w_plane[:].rearrange("p (t m) -> p t m", t=PACK),
+                w_bytes[:].rearrange("p (m t) -> p t m", t=PACK),
+            )
+
+        z_codes = keep.tile([P, S], U32, name="z_codes", align_bytes=64)
+        z_plane = keep.tile([P, S], U8, name="z_plane", align_bytes=64)
+        acc_first = psum.tile([P, PACK, HALF], F32, name="acc_first")
+        acc_lead = psum.tile([P, 1, HALF], F32, name="acc_lead")
+        acc_rest = psum.tile([P, PACK - 1, HALF], F32, name="acc_rest")
+
+        def h2_acc(t, c0):
+            if c0 < HALF:
+                return acc_first[:, t, :]
+            return acc_lead[:, 0, :] if t == 0 else acc_rest[:, t - 1, :]
+
+        def second_product(c0, tiles):
+            for t in tiles:
+                nc.tensor.matmul_mx(
+                    h2_acc(t, c0),
+                    lhsT=w_codes[:, 2 * t * P : 2 * (t + 1) * P].bitcast(FP4X4),
+                    lhsT_scale=w_plane[:, t * P : (t + 1) * P],
+                    rhs=z_codes[:, c0 : c0 + HALF].bitcast(FP8X4),
+                    rhs_scale=z_plane[:, c0 : c0 + HALF],
+                    start=True,
+                    stop=True,
+                )
+
+        for i, (c0, c) in enumerate(starts(PIECES_1)):
+            last = i == len(PIECES_1) - 1
+            z_bf = keep.tile([P, c, PACK], BF16, name="z_bf%d" % i, align_bytes=64)
+            z_f32 = keep.tile([P, PACK, c], F32, name="z_f32%d" % i) if not last else None
+            for t in range(PACK):
+                members = ring.tile([P, c, MEMBERS], F32, name="members", tag="members")
+                largest = ring.tile([P, c], F32, name="largest", tag="largest")
+                nc.scalar.activation(
+                    members[:].rearrange("p c m -> p (c m)"),
+                    h_rows[t][:].indirect(n1_t[:, c0 * MEMBERS // 16 : (c0 + c) * MEMBERS // 16]),
+                    ACT.Copy,
+                )
+                nc.vector.tensor_reduce(largest[:], members[:], AXIS.X, ALU.max)
+                nc.vector.scalar_tensor_tensor(
+                    z_bf[:, :, t] if last else z_f32[:, t, :],
+                    largest[:],
+                    neg_gain[:, t : t + 1],
+                    gained[:, t, c0 : c0 + c],
+                    ALU.mult,
+                    ALU.add,
+                )
+                if i == 0 and t == 1:
+                    deal_w1()
+            if not last:
+                nc.vector.tensor_copy(
+                    z_bf[:].rearrange("p (c i) t -> p c t i", i=4),
+                    z_f32[:].rearrange("p t (c i) -> p c t i", i=4),
+                )
+            nc.vector.quantize_mx(
+                out=z_codes[:, c0 : c0 + c].bitcast(FP8X4),
+                scales=z_plane[:, c0 : c0 + c],
+                in_=z_bf[:].rearrange("p c t -> p (c t)"),
+            )
+            if c0 + c == HALF:
+                second_product(0, range(PACK))
+                nc.vector.tensor_copy(h2_rows[0][:, :HALF], h2_acc(0, 0))
+        second_product(HALF, range(PACK))
+        nc.scalar.activation(h2_rows[0][:, HALF:S], h2_acc(0, HALF), ACT.Copy)
+        for t in range(1, PACK):
+            nc.vector.tensor_copy(h2_rows[t][:, :HALF], h2_acc(t, 0))
+            nc.vector.tensor_copy(h2_rows[t][:, HALF:S], h2_acc(t, HALF))
+
+        y_plane = keep.tile([P, S], U8, name="y_plane", align_bytes=64)
+        out_rows = out_0.rearrange("(p t) j -> p t j", t=PACK)
+        out_words = out_1[0].rearrange("p c r -> p (c r)").bitcast(I32)
+        groups = [
+            (
+                keep.tile([P, PACK, QCOLS], F32, name="y%d" % g),
+                keep.tile([P, QCOLS, PACK], BF16, name="y_bf%d" % g, align_bytes=64),
+                keep.tile([P, QCOLS], U32, name="y_codes%d" % g, align_bytes=64),
+            )
+            for g in range(S // QCOLS)
+        ]
+
+        def finish(c0, c, largest, slope):
+            g, g0 = divmod(c0, QCOLS)
+            y, y_bf, y_codes = groups[g]
+            nc.vector.tensor_tensor(y[:, :, g0 : g0 + c], largest[:], slope[:], ALU.mult)
+            if g0 + c < QCOLS:
+                return
+            cols = slice(g * QCOLS, (g + 1) * QCOLS)
+            nc.sync.dma_start(out_rows[:, :, cols], y[:])
+            nc.vector.tensor_copy(
+                y_bf[:].rearrange("p (c i) t -> p c t i", i=4),
+                y[:].rearrange("p t (c i) -> p c t i", i=4),
+            )
+            nc.vector.quantize_mx(
+                out=y_codes[:].bitcast(FP8X4),
+                scales=y_plane[:, cols],
+                in_=y_bf[:].rearrange("p c t -> p (c t)"),
+            )
+            nc.sync.dma_start(out_words[:, cols], y_codes[:].bitcast(I32))
+
+        waiting = None
+        for c0, c in starts(PIECES_2):
+            members = ring.tile([P, PACK, c, MEMBERS], F32, name="members2", tag="members2")
+            for t in range(PACK):
+                nc.scalar.activation(
+                    members[:, t].rearrange("p c m -> p (c m)"),
+                    h2_rows[t][:].indirect(n2_t[:, c0 * MEMBERS // 16 : (c0 + c) * MEMBERS // 16]),
+                    ACT.Copy,
+                )
+            pairs = members[:].rearrange("p t c m -> p (t c) m")
+            low2 = ring.tile([P, PACK * c, 2], F32, name="low2", tag="low2")
+            high2 = ring.tile([P, PACK * c, 2], F32, name="high2", tag="high2")
+            smallest = ring.tile([P, PACK, c], F32, name="smallest", tag="smallest")
+            largest = ring.tile([P, PACK, c], F32, name="largest2", tag="largest2")
+            rise = ring.tile([P, PACK, c], F32, name="rise", tag="rise")
+            slope = ring.tile([P, PACK, c], F32, name="slope", tag="slope")
+            nc.vector.tensor_tensor(low2[:], pairs[:, :, 0:2], pairs[:, :, 2:4], ALU.min)
+            nc.vector.tensor_tensor(high2[:], pairs[:, :, 0:2], pairs[:, :, 2:4], ALU.max)
+            nc.vector.tensor_tensor(smallest[:].rearrange("p t c -> p (t c)"), low2[:, :, 0], low2[:, :, 1], ALU.min)
+            nc.vector.tensor_tensor(largest[:].rearrange("p t c -> p (t c)"), high2[:, :, 0], high2[:, :, 1], ALU.max)
+            if c0 < HALF:
+                nc.vector.tensor_tensor(rise[:], acc_first[:, :, c0 : c0 + c], smallest[:], ALU.subtract)
+            else:
+                cols = slice(c0 - HALF, c0 - HALF + c)
+                nc.vector.tensor_tensor(rise[:, :1], acc_lead[:, :, cols], smallest[:, :1], ALU.subtract)
+                nc.vector.tensor_tensor(rise[:, 1:], acc_rest[:, :, cols], smallest[:, 1:], ALU.subtract)
+            nc.scalar.activation(slope[:], rise[:], ACT.Tanh)
+            if waiting is not None:
+                finish(*waiting)
+            waiting = (c0, c, largest, slope)
+        finish(*waiting)
+
+        for q in range(4):
+            queue = nc.sync if q % 2 == 0 else nc.scalar
+            queue.dma_start(out_2[0, 4 * q : 4 * q + 4, :].bitcast(I32), y_plane[32 * q : 32 * q + 4, :].bitcast(I32))

@@ -23,8 +23,9 @@ MEMBERS = 4
 HALF = S // 2
 QCOLS = 64
 PIECES_1 = (128, 64, 64)
-PIECES_2 = (64, 64, 64, 32, 32)
+PIECES_2 = (64, 64, 64, 64)
 SPARE = 16
+LEAD = 512
 
 FLOPS = 2 * 2 * 512 * 512 * 256
 
@@ -40,6 +41,7 @@ def tile_picked_pqlaygmaxdgtan_none_po_kernel(
     with ExitStack() as ctx:
         keep = ctx.enter_context(tc.tile_pool(name="keep", bufs=1))
         ring = ctx.enter_context(tc.tile_pool(name="ring", bufs=3))
+        ring2 = ctx.enter_context(tc.tile_pool(name="ring2", bufs=2))
         psum = ctx.enter_context(tc.psum_pool(name="psum", bufs=1))
 
         k1_t = keep.tile([P, H // 16], U16, name="k1_t")
@@ -49,27 +51,29 @@ def tile_picked_pqlaygmaxdgtan_none_po_kernel(
 
         d_bytes = keep.tile([P, TABLE], U8, name="d_bytes")
         x_bytes = keep.tile([P, TABLE], U8, name="x_bytes")
-        planes_1 = keep.tile([P, H + S], U8, name="planes_1", align_bytes=64)
+        moved = keep.tile([P, H + S], U8, name="moved", tag="moved", align_bytes=64)
         nc.vector.memset(d_bytes[:].bitcast(I32), 0)
-        nc.vector.memset(x_bytes[:].bitcast(I32), 0)
-        nc.vector.memset(planes_1[:].bitcast(I32), 0)
+        nc.gpsimd.memset(x_bytes[:].bitcast(I32), 0)
+        nc.vector.memset(moved[:].bitcast(I32), 0)
 
-        d_table = keep.tile([P, TABLE], U32, name="d_table")
-        x_table = keep.tile([P, TABLE], U32, name="x_table")
+        d_table = keep.tile([P, TABLE], U32, name="d_table", tag="d_table")
+        x_table = keep.tile([P, TABLE], U32, name="x_table", tag="x_table", align_bytes=64)
         gain = keep.tile([P, PACK], F32, name="gain")
+        d_in = d_words[0].rearrange("p n t -> p (n t)").bitcast(I32)
         nc.sync.dma_start(k1_t[:], k1)
+        nc.sync.dma_start(d_table[:, :LEAD].bitcast(I32), d_in[:, :LEAD])
+        nc.sync.dma_start(d_bytes[0:P:8, :].bitcast(I32), d_scales[0].bitcast(I32))
+        nc.sync.dma_start(x_bytes[0:P:8, :].bitcast(I32), x_scales[0].bitcast(I32))
         nc.sync.dma_start(offs_t[:], offs)
+        nc.sync.dma_start(d_table[:, LEAD:].bitcast(I32), d_in[:, LEAD:])
+        nc.sync.dma_start(x_table[:].bitcast(I32), x_words[0].rearrange("p n t -> p (n t)").bitcast(I32))
         nc.sync.dma_start(n1_t[:], n1)
         nc.sync.dma_start(n2_t[:], n2)
         nc.sync.dma_start(gain[:], gn.rearrange("(p t) o -> p (t o)", t=PACK))
-        nc.scalar.dma_start(d_bytes[0:P:8, :].bitcast(I32), d_scales[0].bitcast(I32))
-        nc.scalar.dma_start(x_bytes[0:P:8, :].bitcast(I32), x_scales[0].bitcast(I32))
-        nc.sync.dma_start(d_table[:].bitcast(I32), d_words[0].rearrange("p n t -> p (n t)").bitcast(I32))
-        nc.sync.dma_start(x_table[:].bitcast(I32), x_words[0].rearrange("p n t -> p (n t)").bitcast(I32))
 
         wide_1 = MEMBERS * max(PIECES_1) + SPARE
-        wide_2 = MEMBERS * max(PIECES_2) + SPARE
         h_rows = [keep.tile([P, wide_1], F32, name="h_rows%d" % t) for t in range(PACK)]
+        wide_2 = MEMBERS * max(PIECES_2) + SPARE
         h2_rows = [keep.tile([P, wide_2], F32, name="h2_rows%d" % t) for t in range(PACK)]
         for t in range(PACK):
             nc.vector.memset(h_rows[t][:, S:], 0.0)
@@ -78,21 +82,15 @@ def tile_picked_pqlaygmaxdgtan_none_po_kernel(
         neg_gain = keep.tile([P, PACK], F32, name="neg_gain")
         nc.scalar.activation(neg_gain[:], gain[:], ACT.Copy, scale=-1.0)
 
-        d_bytes_picked = keep.tile([P, H], U8, name="d_bytes_picked")
-        x_bytes_picked = keep.tile([P, S], U8, name="x_bytes_picked")
-        staged = keep.tile([P, H + S], U8, name="staged", tag="staged", align_bytes=64)
-        nc.vector.tensor_copy(d_bytes_picked[:], d_bytes[:].indirect(k1_t[:]))
-        nc.vector.tensor_copy(x_bytes_picked[:], x_bytes[:].indirect(offs_t[:]))
-        nc.vector.tensor_copy(
-            staged[:, :H].rearrange("p (t m) -> p t m", t=PACK),
-            d_bytes_picked[:].rearrange("p (m t) -> p t m", t=PACK),
-        )
-        nc.vector.tensor_copy(staged[:, H:], x_bytes_picked[:])
+        picked_bytes = keep.tile([P, H + S], U8, name="picked_bytes", tag="picked_bytes")
+        nc.vector.tensor_copy(picked_bytes[:, :H], d_bytes[:].indirect(k1_t[:]))
+        nc.vector.tensor_copy(picked_bytes[:, H:], x_bytes[:].indirect(offs_t[:]))
         for r in range(4):
-            nc.sync.dma_start(planes_1[r:P:32, :].bitcast(I32), staged[8 * r : P : 32, :].bitcast(I32))
+            nc.scalar.dma_start(moved[r:P:32, :].bitcast(I32), picked_bytes[8 * r : P : 32, :].bitcast(I32))
 
         d_picked = keep.tile([P, H], U32, name="d_picked")
         d_codes = keep.tile([P, H], U32, name="d_codes", align_bytes=64)
+        d_plane = keep.tile([P, H], U8, name="d_plane", align_bytes=64)
         x_codes = keep.tile([P, S], U32, name="x_codes", align_bytes=64)
         nc.vector.tensor_copy(d_picked[:], d_table[:].indirect(k1_t[:]))
         nc.vector.tensor_copy(
@@ -100,6 +98,10 @@ def tile_picked_pqlaygmaxdgtan_none_po_kernel(
             d_picked[:].bitcast(I32).rearrange("p (m t) -> p t m", t=PACK),
         )
         nc.vector.tensor_copy(x_codes[:], x_table[:].indirect(offs_t[:]))
+        d_plane_out = d_plane[:].rearrange("p (t m) -> p t m", t=PACK)
+        d_plane_in = moved[:, :H].rearrange("p (m t) -> p t m", t=PACK)
+        nc.vector.tensor_copy(d_plane_out[:, :1], d_plane_in[:, :1])
+        nc.vector.tensor_copy(d_plane_out[:, 1:], d_plane_in[:, 1:])
 
         gained = keep.tile([P, PACK, S], F32, name="gained")
         for t in range(PACK):
@@ -107,9 +109,9 @@ def tile_picked_pqlaygmaxdgtan_none_po_kernel(
             nc.tensor.matmul_mx(
                 acc[:],
                 lhsT=d_codes[:, t * P : (t + 1) * P].bitcast(FP8X4),
-                lhsT_scale=planes_1[:, t * P : (t + 1) * P],
+                lhsT_scale=d_plane[:, t * P : (t + 1) * P],
                 rhs=x_codes[:].bitcast(FP8X4),
-                rhs_scale=planes_1[:, H:],
+                rhs_scale=moved[:, H:],
                 start=True,
                 stop=True,
             )
@@ -120,10 +122,10 @@ def tile_picked_pqlaygmaxdgtan_none_po_kernel(
         for t in range(PACK):
             nc.vector.tensor_scalar(gained[:, t, :], h_rows[t][:, :S], gain[:, t : t + 1], None, ALU.mult)
 
-        w_raw = keep.tile([P, 2 * H], U8, name="w_raw", tag="staged", align_bytes=64)
-        w_bytes = keep.tile([P, H], U8, name="w_bytes", tag="d_bytes_picked")
-        w_codes = keep.tile([P, 2 * H], U8, name="w_codes", align_bytes=64)
-        w_plane = keep.tile([P, H], U8, name="w_plane", align_bytes=64)
+        w_raw = keep.tile([P, 2 * H], U8, name="w_raw", tag="picked_bytes")
+        w_bytes = keep.tile([P, H], U8, name="w_bytes", tag="d_table")
+        w_codes = keep.tile([P, 2 * H], U8, name="w_codes", tag="x_table", align_bytes=64)
+        w_plane = keep.tile([P, H], U8, name="w_plane", tag="moved", align_bytes=64)
         nc.sync.dma_start(w_raw[:].bitcast(I32), w1_words[0].bitcast(I32))
         nc.vector.memset(w_bytes[:].bitcast(I32), 0)
         for q in range(4):
@@ -141,19 +143,12 @@ def tile_picked_pqlaygmaxdgtan_none_po_kernel(
 
         z_codes = keep.tile([P, S], U32, name="z_codes", align_bytes=64)
         z_plane = keep.tile([P, S], U8, name="z_plane", align_bytes=64)
-        acc_first = psum.tile([P, PACK, HALF], F32, name="acc_first")
-        acc_lead = psum.tile([P, 1, HALF], F32, name="acc_lead")
-        acc_rest = psum.tile([P, PACK - 1, HALF], F32, name="acc_rest")
+        h2_acc = [psum.tile([P, S], F32, name="h2_acc%d" % t) for t in range(PACK)]
 
-        def h2_acc(t, c0):
-            if c0 < HALF:
-                return acc_first[:, t, :]
-            return acc_lead[:, 0, :] if t == 0 else acc_rest[:, t - 1, :]
-
-        def second_product(c0, tiles):
-            for t in tiles:
+        def second_product(c0):
+            for t in range(PACK):
                 nc.tensor.matmul_mx(
-                    h2_acc(t, c0),
+                    h2_acc[t][:, c0 : c0 + HALF],
                     lhsT=w_codes[:, 2 * t * P : 2 * (t + 1) * P].bitcast(FP4X4),
                     lhsT_scale=w_plane[:, t * P : (t + 1) * P],
                     rhs=z_codes[:, c0 : c0 + HALF].bitcast(FP8X4),
@@ -162,27 +157,28 @@ def tile_picked_pqlaygmaxdgtan_none_po_kernel(
                     stop=True,
                 )
 
+        def fetch(out, window, entries, c0, c):
+            nc.scalar.activation(
+                out.rearrange("p c m -> p (c m)"),
+                window[:].indirect(entries[:, c0 * MEMBERS // 16 : (c0 + c) * MEMBERS // 16]),
+                ACT.Copy,
+            )
+
+        def make_z(out, largest, t, c0, c):
+            nc.vector.scalar_tensor_tensor(
+                out, largest, neg_gain[:, t : t + 1], gained[:, t, c0 : c0 + c], ALU.mult, ALU.add
+            )
+
         for i, (c0, c) in enumerate(starts(PIECES_1)):
-            last = i == len(PIECES_1) - 1
             z_bf = keep.tile([P, c, PACK], BF16, name="z_bf%d" % i, align_bytes=64)
-            z_f32 = keep.tile([P, PACK, c], F32, name="z_f32%d" % i) if not last else None
+            last = c0 + c == S
+            z_f32 = None if last else keep.tile([P, PACK, c], F32, name="z_f32%d" % i)
             for t in range(PACK):
                 members = ring.tile([P, c, MEMBERS], F32, name="members", tag="members")
                 largest = ring.tile([P, c], F32, name="largest", tag="largest")
-                nc.scalar.activation(
-                    members[:].rearrange("p c m -> p (c m)"),
-                    h_rows[t][:].indirect(n1_t[:, c0 * MEMBERS // 16 : (c0 + c) * MEMBERS // 16]),
-                    ACT.Copy,
-                )
+                fetch(members[:], h_rows[t], n1_t, c0, c)
                 nc.vector.tensor_reduce(largest[:], members[:], AXIS.X, ALU.max)
-                nc.vector.scalar_tensor_tensor(
-                    z_bf[:, :, t] if last else z_f32[:, t, :],
-                    largest[:],
-                    neg_gain[:, t : t + 1],
-                    gained[:, t, c0 : c0 + c],
-                    ALU.mult,
-                    ALU.add,
-                )
+                make_z(z_bf[:, :, t] if last else z_f32[:, t, :], largest[:], t, c0, c)
                 if i == 0 and t == 1:
                     deal_w1()
             if not last:
@@ -196,76 +192,76 @@ def tile_picked_pqlaygmaxdgtan_none_po_kernel(
                 in_=z_bf[:].rearrange("p c t -> p (c t)"),
             )
             if c0 + c == HALF:
-                second_product(0, range(PACK))
-                nc.vector.tensor_copy(h2_rows[0][:, :HALF], h2_acc(0, 0))
-        second_product(HALF, range(PACK))
-        nc.scalar.activation(h2_rows[0][:, HALF:S], h2_acc(0, HALF), ACT.Copy)
+                second_product(0)
+                nc.vector.tensor_copy(h2_rows[0][:, :HALF], h2_acc[0][:, :HALF])
+        second_product(HALF)
+        nc.scalar.activation(h2_rows[0][:, HALF:S], h2_acc[0][:, HALF:], ACT.Copy)
         for t in range(1, PACK):
-            nc.vector.tensor_copy(h2_rows[t][:, :HALF], h2_acc(t, 0))
-            nc.vector.tensor_copy(h2_rows[t][:, HALF:S], h2_acc(t, HALF))
+            nc.vector.tensor_copy(h2_rows[t][:, :S], h2_acc[t][:])
+        h2_all = keep.tile([P, PACK, S], F32, name="h2_all")
+        for t in range(PACK):
+            nc.vector.tensor_copy(h2_all[:, t, :], h2_rows[t][:, :S])
 
         y_plane = keep.tile([P, S], U8, name="y_plane", align_bytes=64)
         out_rows = out_0.rearrange("(p t) j -> p t j", t=PACK)
         out_words = out_1[0].rearrange("p c r -> p (c r)").bitcast(I32)
-        groups = [
-            (
-                keep.tile([P, PACK, QCOLS], F32, name="y%d" % g),
-                keep.tile([P, QCOLS, PACK], BF16, name="y_bf%d" % g, align_bytes=64),
-                keep.tile([P, QCOLS], U32, name="y_codes%d" % g, align_bytes=64),
-            )
-            for g in range(S // QCOLS)
-        ]
 
-        def finish(c0, c, largest, slope):
-            g, g0 = divmod(c0, QCOLS)
-            y, y_bf, y_codes = groups[g]
-            nc.vector.tensor_tensor(y[:, :, g0 : g0 + c], largest[:], slope[:], ALU.mult)
-            if g0 + c < QCOLS:
-                return
-            cols = slice(g * QCOLS, (g + 1) * QCOLS)
-            nc.sync.dma_start(out_rows[:, :, cols], y[:])
+        def product(piece):
+            c0, c, largest, slope, y, y_bf = piece
+            nc.vector.tensor_tensor(y[:], largest[:], slope[:], ALU.mult)
+            nc.sync.dma_start(out_rows[:, :, c0 : c0 + c], y[:])
+
+        def round_y(piece):
+            c0, c, largest, slope, y, y_bf = piece
             nc.vector.tensor_copy(
                 y_bf[:].rearrange("p (c i) t -> p c t i", i=4),
                 y[:].rearrange("p t (c i) -> p c t i", i=4),
             )
+
+        def quantise(piece):
+            c0, c, largest, slope, y, y_bf = piece
+            y_codes = keep.tile([P, c], U32, name="y_codes%d" % c0, align_bytes=64)
             nc.vector.quantize_mx(
                 out=y_codes[:].bitcast(FP8X4),
-                scales=y_plane[:, cols],
+                scales=y_plane[:, c0 : c0 + c],
                 in_=y_bf[:].rearrange("p c t -> p (c t)"),
             )
-            nc.sync.dma_start(out_words[:, cols], y_codes[:].bitcast(I32))
+            nc.sync.dma_start(out_words[:, c0 : c0 + c], y_codes[:].bitcast(I32))
 
         waiting = None
         for c0, c in starts(PIECES_2):
-            members = ring.tile([P, PACK, c, MEMBERS], F32, name="members2", tag="members2")
+            work = ring2.tile([P, PACK * c * (MEMBERS + 1)], F32, name="work", tag="work")
+            members = work[:, : PACK * c * MEMBERS].rearrange("p (t c m) -> p t c m", t=PACK, m=MEMBERS)
+            rise = work[:, PACK * c * MEMBERS :].rearrange("p (t c) -> p t c", t=PACK)
             for t in range(PACK):
-                nc.scalar.activation(
-                    members[:, t].rearrange("p c m -> p (c m)"),
-                    h2_rows[t][:].indirect(n2_t[:, c0 * MEMBERS // 16 : (c0 + c) * MEMBERS // 16]),
-                    ACT.Copy,
-                )
-            pairs = members[:].rearrange("p t c m -> p (t c) m")
+                fetch(members[:, t], h2_rows[t], n2_t, c0, c)
+            pairs = members.rearrange("p t c m -> p (t c) m")
             low2 = ring.tile([P, PACK * c, 2], F32, name="low2", tag="low2")
             high2 = ring.tile([P, PACK * c, 2], F32, name="high2", tag="high2")
             smallest = ring.tile([P, PACK, c], F32, name="smallest", tag="smallest")
             largest = ring.tile([P, PACK, c], F32, name="largest2", tag="largest2")
-            rise = ring.tile([P, PACK, c], F32, name="rise", tag="rise")
             slope = ring.tile([P, PACK, c], F32, name="slope", tag="slope")
-            nc.vector.tensor_tensor(low2[:], pairs[:, :, 0:2], pairs[:, :, 2:4], ALU.min)
-            nc.vector.tensor_tensor(high2[:], pairs[:, :, 0:2], pairs[:, :, 2:4], ALU.max)
+            y = keep.tile([P, PACK, c], F32, name="y%d" % c0)
+            y_bf = keep.tile([P, c, PACK], BF16, name="y_bf%d" % c0, align_bytes=64)
+            for part in (slice(0, 2 * c), slice(2 * c, 4 * c)):
+                nc.vector.tensor_tensor(low2[:, part], pairs[:, part, 0:2], pairs[:, part, 2:4], ALU.min)
+                nc.vector.tensor_tensor(high2[:, part], pairs[:, part, 0:2], pairs[:, part, 2:4], ALU.max)
             nc.vector.tensor_tensor(smallest[:].rearrange("p t c -> p (t c)"), low2[:, :, 0], low2[:, :, 1], ALU.min)
-            nc.vector.tensor_tensor(largest[:].rearrange("p t c -> p (t c)"), high2[:, :, 0], high2[:, :, 1], ALU.max)
-            if c0 < HALF:
-                nc.vector.tensor_tensor(rise[:], acc_first[:, :, c0 : c0 + c], smallest[:], ALU.subtract)
-            else:
-                cols = slice(c0 - HALF, c0 - HALF + c)
-                nc.vector.tensor_tensor(rise[:, :1], acc_lead[:, :, cols], smallest[:, :1], ALU.subtract)
-                nc.vector.tensor_tensor(rise[:, 1:], acc_rest[:, :, cols], smallest[:, 1:], ALU.subtract)
-            nc.scalar.activation(slope[:], rise[:], ACT.Tanh)
             if waiting is not None:
-                finish(*waiting)
-            waiting = (c0, c, largest, slope)
-        finish(*waiting)
+                product(waiting)
+            nc.vector.tensor_tensor(rise, h2_all[:, :, c0 : c0 + c], smallest[:], ALU.subtract)
+            nc.scalar.activation(slope[:], rise, ACT.Tanh)
+            if waiting is not None:
+                round_y(waiting)
+            nc.vector.tensor_tensor(largest[:].rearrange("p t c -> p (t c)"), high2[:, :, 0], high2[:, :, 1], ALU.max)
+            if waiting is not None:
+                quantise(waiting)
+            waiting = (c0, c, largest, slope, y, y_bf)
+        nc.vector.tensor_tensor(
+            y_bf[:], largest[:].rearrange("p t c -> p c t"), slope[:].rearrange("p t c -> p c t"), ALU.mult
+        )
+        product(waiting)
+        quantise(waiting)
 
         for q in range(4):
             queue = nc.sync if q % 2 == 0 else nc.scalar

@@ -79,8 +79,6 @@ def tile_picked_pqlaygmaxdgtan_none_po_kernel(
             nc.vector.memset(h_rows[t][:, S:], 0.0)
             nc.vector.memset(h2_rows[t][:, S:], 0.0)
 
-        neg_gain = keep.tile([P, PACK], F32, name="neg_gain")
-        nc.scalar.activation(neg_gain[:], gain[:], ACT.Copy, scale=-1.0)
 
         picked_bytes = keep.tile([P, H + S], U8, name="picked_bytes", tag="picked_bytes")
         nc.vector.tensor_copy(picked_bytes[:, :H], d_bytes[:].indirect(k1_t[:]))
@@ -116,9 +114,9 @@ def tile_picked_pqlaygmaxdgtan_none_po_kernel(
                 stop=True,
             )
             if t == 0:
-                nc.scalar.activation(h_rows[t][:, :S], acc[:], ACT.Copy, scale=0.0625)
+                nc.scalar.activation(h_rows[t][:, :S], acc[:], ACT.Copy, scale=-0.0625)
             else:
-                nc.vector.tensor_scalar(h_rows[t][:, :S], acc[:], 0.0625, None, ALU.mult)
+                nc.vector.tensor_scalar(h_rows[t][:, :S], acc[:], -0.0625, None, ALU.mult)
         for t in range(PACK):
             nc.vector.tensor_scalar(gained[:, t, :], h_rows[t][:, :S], gain[:, t : t + 1], None, ALU.mult)
 
@@ -166,7 +164,7 @@ def tile_picked_pqlaygmaxdgtan_none_po_kernel(
 
         def make_z(out, largest, t, c0, c):
             nc.vector.scalar_tensor_tensor(
-                out, largest, neg_gain[:, t : t + 1], gained[:, t, c0 : c0 + c], ALU.mult, ALU.add
+                out, largest, gain[:, t : t + 1], gained[:, t, c0 : c0 + c], ALU.mult, ALU.subtract
             )
 
         for i, (c0, c) in enumerate(starts(PIECES_1)):
@@ -177,7 +175,7 @@ def tile_picked_pqlaygmaxdgtan_none_po_kernel(
                 members = ring.tile([P, c, MEMBERS], F32, name="members", tag="members")
                 largest = ring.tile([P, c], F32, name="largest", tag="largest")
                 fetch(members[:], h_rows[t], n1_t, c0, c)
-                nc.vector.tensor_reduce(largest[:], members[:], AXIS.X, ALU.max)
+                nc.vector.tensor_reduce(largest[:], members[:], AXIS.X, ALU.min)
                 make_z(z_bf[:, :, t] if last else z_f32[:, t, :], largest[:], t, c0, c)
                 if i == 0 and t == 1:
                     deal_w1()
@@ -232,13 +230,13 @@ def tile_picked_pqlaygmaxdgtan_none_po_kernel(
         for c0, c in starts(PIECES_2):
             work = ring2.tile([P, PACK * c * (MEMBERS + 1)], F32, name="work", tag="work")
             members = work[:, : PACK * c * MEMBERS].rearrange("p (t c m) -> p t c m", t=PACK, m=MEMBERS)
-            rise = work[:, PACK * c * MEMBERS :].rearrange("p (t c) -> p t c", t=PACK)
+            smallest = work[:, PACK * c * MEMBERS :]
             for t in range(PACK):
                 fetch(members[:, t], h2_rows[t], n2_t, c0, c)
             pairs = members.rearrange("p t c m -> p (t c) m")
             low2 = ring.tile([P, PACK * c, 2], F32, name="low2", tag="low2")
             high2 = ring.tile([P, PACK * c, 2], F32, name="high2", tag="high2")
-            smallest = ring.tile([P, PACK, c], F32, name="smallest", tag="smallest")
+            rise = ring.tile([P, PACK, c], F32, name="rise", tag="rise")
             largest = ring.tile([P, PACK, c], F32, name="largest2", tag="largest2")
             slope = ring.tile([P, PACK, c], F32, name="slope", tag="slope")
             y = keep.tile([P, PACK, c], F32, name="y%d" % c0)
@@ -246,11 +244,13 @@ def tile_picked_pqlaygmaxdgtan_none_po_kernel(
             for part in (slice(0, 2 * c), slice(2 * c, 4 * c)):
                 nc.vector.tensor_tensor(low2[:, part], pairs[:, part, 0:2], pairs[:, part, 2:4], ALU.min)
                 nc.vector.tensor_tensor(high2[:, part], pairs[:, part, 0:2], pairs[:, part, 2:4], ALU.max)
-            nc.vector.tensor_tensor(smallest[:].rearrange("p t c -> p (t c)"), low2[:, :, 0], low2[:, :, 1], ALU.min)
+            nc.vector.tensor_tensor(smallest, low2[:, :, 0], low2[:, :, 1], ALU.min)
             if waiting is not None:
                 product(waiting)
-            nc.vector.tensor_tensor(rise, h2_all[:, :, c0 : c0 + c], smallest[:], ALU.subtract)
-            nc.scalar.activation(slope[:], rise, ACT.Tanh)
+            nc.vector.tensor_tensor(
+                rise[:], h2_all[:, :, c0 : c0 + c], smallest.rearrange("p (t c) -> p t c", t=PACK), ALU.subtract
+            )
+            nc.scalar.activation(slope[:], rise[:], ACT.Tanh)
             if waiting is not None:
                 round_y(waiting)
             nc.vector.tensor_tensor(largest[:].rearrange("p t c -> p (t c)"), high2[:, :, 0], high2[:, :, 1], ALU.max)

@@ -42,6 +42,7 @@ def tile_picked_pqlaygmaxdgtan_none_po_kernel(
         keep = ctx.enter_context(tc.tile_pool(name="keep", bufs=1))
         ring = ctx.enter_context(tc.tile_pool(name="ring", bufs=3))
         ring2 = ctx.enter_context(tc.tile_pool(name="ring2", bufs=2))
+        ring4 = ctx.enter_context(tc.tile_pool(name="ring4", bufs=4))
         psum = ctx.enter_context(tc.psum_pool(name="psum", bufs=1))
 
         k1_t = keep.tile([P, H // 16], U16, name="k1_t")
@@ -53,7 +54,7 @@ def tile_picked_pqlaygmaxdgtan_none_po_kernel(
         x_bytes = keep.tile([P, TABLE], U8, name="x_bytes")
         moved = keep.tile([P, H + S], U8, name="moved", tag="moved", align_bytes=64)
         nc.vector.memset(d_bytes[:].bitcast(I32), 0)
-        nc.gpsimd.memset(x_bytes[:].bitcast(I32), 0)
+        nc.vector.memset(x_bytes[:].bitcast(I32), 0)
         nc.vector.memset(moved[:].bitcast(I32), 0)
 
         d_table = keep.tile([P, TABLE], U32, name="d_table", tag="d_table")
@@ -172,7 +173,7 @@ def tile_picked_pqlaygmaxdgtan_none_po_kernel(
             last = c0 + c == S
             z_f32 = None if last else keep.tile([P, PACK, c], F32, name="z_f32%d" % i)
             for t in range(PACK):
-                members = ring.tile([P, c, MEMBERS], F32, name="members", tag="members")
+                members = ring4.tile([P, c, MEMBERS], F32, name="members", tag="members")
                 largest = ring.tile([P, c], F32, name="largest", tag="largest")
                 fetch(members[:], h_rows[t], n1_t, c0, c)
                 nc.vector.tensor_reduce(largest[:], members[:], AXIS.X, ALU.min)

from contextlib import ExitStack

import concourse.mybir as mybir

F32 = mybir.dt.float32
BF16 = mybir.dt.bfloat16
I32 = mybir.dt.int32
U32 = mybir.dt.uint32
U16 = mybir.dt.uint16
U8 = mybir.dt.uint8
FP8X4 = mybir.dt.float8_e4m3fn_x4
FP4X4 = mybir.dt.float4_e2m1fn_x4
ALU = mybir.AluOpType
ACT = mybir.ActivationFunctionType
AXIS = mybir.AxisListType

P = 128
PACK = 4
TABLE = 2048
S = 256
H = 512
MEMBERS = 4
HALF = S // 2
QCOLS = 64
PIECES_1 = (128, 64, 64)
PIECES_2 = (64, 64, 64, 64)
SPARE = 16
LEAD = 512

FLOPS = 2 * 2 * 512 * 512 * 256


def starts(widths):
    return [(sum(widths[:i]), w) for i, w in enumerate(widths)]


def tile_picked_pqlaygmaxdgtan_none_po_kernel(
    tc, x_words, x_scales, d_words, d_scales, gn, w1_words, w1_scales, offs, k1, n1, n2, out_0, out_1, out_2
):
    nc = tc.nc
    with ExitStack() as ctx:
        keep = ctx.enter_context(tc.tile_pool(name="keep", bufs=1))
        ring = ctx.enter_context(tc.tile_pool(name="ring", bufs=3))
        ring2 = ctx.enter_context(tc.tile_pool(name="ring2", bufs=2))
        ring4 = ctx.enter_context(tc.tile_pool(name="ring4", bufs=4))
        psum = ctx.enter_context(tc.psum_pool(name="psum", bufs=1))

        k1_t = keep.tile([P, H // 16], U16, name="k1_t")
        offs_t = keep.tile([P, S // 16], U16, name="offs_t")
        n1_t = keep.tile([P, MEMBERS * S // 16], U16, name="n1_t")
        n2_t = keep.tile([P, MEMBERS * S // 16], U16, name="n2_t")

        d_bytes = keep.tile([P, TABLE], U8, name="d_bytes")
        x_bytes = keep.tile([P, TABLE], U8, name="x_bytes")
        moved = keep.tile([P, H + S], U8, name="moved", tag="moved", align_bytes=64)
        nc.vector.memset(d_bytes[:].bitcast(I32), 0)
        nc.vector.memset(x_bytes[:].bitcast(I32), 0)
        nc.vector.memset(moved[:].bitcast(I32), 0)

        d_table = keep.tile([P, TABLE], U32, name="d_table", tag="d_table")
        x_table = keep.tile([P, TABLE], U32, name="x_table", tag="x_table", align_bytes=64)
        gain = keep.tile([P, PACK], F32, name="gain")
        d_in = d_words[0].rearrange("p n t -> p (n t)").bitcast(I32)
        nc.sync.dma_start(k1_t[:], k1)
        nc.sync.dma_start(d_table[:, :LEAD].bitcast(I32), d_in[:, :LEAD])
        nc.sync.dma_start(d_bytes[0:P:8, :].bitcast(I32), d_scales[0].bitcast(I32))
        nc.sync.dma_start(x_bytes[0:P:8, :].bitcast(I32), x_scales[0].bitcast(I32))
        nc.sync.dma_start(offs_t[:], offs)
        nc.sync.dma_start(d_table[:, LEAD:].bitcast(I32), d_in[:, LEAD:])
        nc.sync.dma_start(x_table[:].bitcast(I32), x_words[0].rearrange("p n t -> p (n t)").bitcast(I32))
        nc.sync.dma_start(n1_t[:], n1)
        nc.sync.dma_start(n2_t[:], n2)
        nc.sync.dma_start(gain[:], gn.rearrange("(p t) o -> p (t o)", t=PACK))

        wide_1 = MEMBERS * max(PIECES_1) + SPARE
        h_rows = [keep.tile([P, wide_1], F32, name="h_rows%d" % t) for t in range(PACK)]
        wide_2 = MEMBERS * max(PIECES_2) + SPARE
        h2_rows = [keep.tile([P, wide_2], F32, name="h2_rows%d" % t) for t in range(PACK)]
        for t in range(PACK):
            nc.vector.memset(h_rows[t][:, S:], 0.0)
            nc.vector.memset(h2_rows[t][:, S:], 0.0)


        picked_bytes = keep.tile([P, H + S], U8, name="picked_bytes", tag="picked_bytes")
        nc.vector.tensor_copy(picked_bytes[:, :H], d_bytes[:].indirect(k1_t[:]))
        nc.vector.tensor_copy(picked_bytes[:, H:], x_bytes[:].indirect(offs_t[:]))
        for r in range(4):
            nc.scalar.dma_start(moved[r:P:32, :].bitcast(I32), picked_bytes[8 * r : P : 32, :].bitcast(I32))

        d_picked = keep.tile([P, H], U32, name="d_picked")
        d_codes = keep.tile([P, H], U32, name="d_codes", align_bytes=64)
        d_plane = keep.tile([P, H], U8, name="d_plane", align_bytes=64)
        x_codes = keep.tile([P, S], U32, name="x_codes", align_bytes=64)
        nc.vector.tensor_copy(d_picked[:], d_table[:].indirect(k1_t[:]))
        nc.vector.tensor_copy(
            d_codes[:].bitcast(I32).rearrange("p (t m) -> p t m", t=PACK),
            d_picked[:].bitcast(I32).rearrange("p (m t) -> p t m", t=PACK),
        )
        nc.vector.tensor_copy(x_codes[:], x_table[:].indirect(offs_t[:]))
        d_plane_out = d_plane[:].rearrange("p (t m) -> p t m", t=PACK)
        d_plane_in = moved[:, :H].rearrange("p (m t) -> p t m", t=PACK)
        nc.vector.tensor_copy(d_plane_out[:, :1], d_plane_in[:, :1])
        nc.vector.tensor_copy(d_plane_out[:, 1:], d_plane_in[:, 1:])

        gained = keep.tile([P, PACK, S], F32, name="gained")
        for t in range(PACK):
            acc = psum.tile([P, S], F32, name="h_acc%d" % t)
            nc.tensor.matmul_mx(
                acc[:],
                lhsT=d_codes[:, t * P : (t + 1) * P].bitcast(FP8X4),
                lhsT_scale=d_plane[:, t * P : (t + 1) * P],
                rhs=x_codes[:].bitcast(FP8X4),
                rhs_scale=moved[:, H:],
                start=True,
                stop=True,
            )
            if t == 0:
                nc.scalar.activation(h_rows[t][:, :S], acc[:], ACT.Copy, scale=-0.0625)
            else:
                nc.vector.tensor_scalar(h_rows[t][:, :S], acc[:], -0.0625, None, ALU.mult)
        for t in range(PACK):
            nc.vector.tensor_scalar(gained[:, t, :], h_rows[t][:, :S], gain[:, t : t + 1], None, ALU.mult)

        w_raw = keep.tile([P, 2 * H], U8, name="w_raw", tag="picked_bytes")
        w_bytes = keep.tile([P, H], U8, name="w_bytes", tag="d_table")
        w_codes = keep.tile([P, 2 * H], U8, name="w_codes", tag="x_table", align_bytes=64)
        w_plane = keep.tile([P, H], U8, name="w_plane", tag="moved", align_bytes=64)
        nc.sync.dma_start(w_raw[:].bitcast(I32), w1_words[0].bitcast(I32))
        nc.vector.memset(w_bytes[:].bitcast(I32), 0)
        for q in range(4):
            nc.sync.dma_start(w_bytes[32 * q : 32 * q + 4, :].bitcast(I32), w1_scales[0, 4 * q : 4 * q + 4, :].bitcast(I32))

        def deal_w1():
            nc.vector.tensor_copy(
                w_codes[:].rearrange("p (t m b) -> p t m b", t=PACK, b=2),
                w_raw[:].rearrange("p (m t b) -> p t m b", t=PACK, b=2),
            )
            nc.vector.tensor_copy(
                w_plane[:].rearrange("p (t m) -> p t m", t=PACK),
                w_bytes[:].rearrange("p (m t) -> p t m", t=PACK),
            )

        z_codes = keep.tile([P, S], U32, name="z_codes", align_bytes=64)
        z_plane = keep.tile([P, S], U8, name="z_plane", align_bytes=64)
        h2_acc = [psum.tile([P, S], F32, name="h2_acc%d" % t) for t in range(PACK)]

        def second_product(c0):
            for t in range(PACK):
                nc.tensor.matmul_mx(
                    h2_acc[t][:, c0 : c0 + HALF],
                    lhsT=w_codes[:, 2 * t * P : 2 * (t + 1) * P].bitcast(FP4X4),
                    lhsT_scale=w_plane[:, t * P : (t + 1) * P],
                    rhs=z_codes[:, c0 : c0 + HALF].bitcast(FP8X4),
                    rhs_scale=z_plane[:, c0 : c0 + HALF],
                    start=True,
                    stop=True,
                )

        def fetch(out, window, entries, c0, c):
            nc.scalar.activation(
                out.rearrange("p c m -> p (c m)"),
                window[:].indirect(entries[:, c0 * MEMBERS // 16 : (c0 + c) * MEMBERS // 16]),
                ACT.Copy,
            )

        def make_z(out, largest, t, c0, c):
            nc.vector.scalar_tensor_tensor(
                out, largest, gain[:, t : t + 1], gained[:, t, c0 : c0 + c], ALU.mult, ALU.subtract
            )

        for i, (c0, c) in enumerate(starts(PIECES_1)):
            z_bf = keep.tile([P, c, PACK], BF16, name="z_bf%d" % i, align_bytes=64)
            last = c0 + c == S
            z_f32 = None if last else keep.tile([P, PACK, c], F32, name="z_f32%d" % i)
            for t in range(PACK):
                members = ring4.tile([P, c, MEMBERS], F32, name="members", tag="members")
                largest = ring.tile([P, c], F32, name="largest", tag="largest")
                fetch(members[:], h_rows[t], n1_t, c0, c)
                nc.vector.tensor_reduce(largest[:], members[:], AXIS.X, ALU.min)
                make_z(z_bf[:, :, t] if last else z_f32[:, t, :], largest[:], t, c0, c)
                if i == 0 and t == 1:
                    deal_w1()
            if not last:
                nc.vector.tensor_copy(
                    z_bf[:].rearrange("p (c i) t -> p c t i", i=4),
                    z_f32[:].rearrange("p t (c i) -> p c t i", i=4),
                )
            nc.vector.quantize_mx(
                out=z_codes[:, c0 : c0 + c].bitcast(FP8X4),
                scales=z_plane[:, c0 : c0 + c],
                in_=z_bf[:].rearrange("p c t -> p (c t)"),
            )
            if c0 + c == HALF:
                second_product(0)
                nc.vector.tensor_copy(h2_rows[0][:, :HALF], h2_acc[0][:, :HALF])
        second_product(HALF)
        nc.scalar.activation(h2_rows[0][:, HALF:S], h2_acc[0][:, HALF:], ACT.Copy)
        for t in range(1, PACK):
            nc.vector.tensor_copy(h2_rows[t][:, :S], h2_acc[t][:])
        h2_all = keep.tile([P, PACK, S], F32, name="h2_all")
        for t in range(PACK):
            nc.vector.tensor_copy(h2_all[:, t, :], h2_rows[t][:, :S])

        y_plane = keep.tile([P, S], U8, name="y_plane", align_bytes=64)
        out_rows = out_0.rearrange("(p t) j -> p t j", t=PACK)
        out_words = out_1[0].rearrange("p c r -> p (c r)").bitcast(I32)

        def product(piece):
            c0, c, largest, slope, y, y_bf = piece
            nc.vector.tensor_tensor(y[:], largest[:], slope[:], ALU.mult)
            nc.sync.dma_start(out_rows[:, :, c0 : c0 + c], y[:])

        def round_y(piece):
            c0, c, largest, slope, y, y_bf = piece
            nc.vector.tensor_copy(
                y_bf[:].rearrange("p (c i) t -> p c t i", i=4),
                y[:].rearrange("p t (c i) -> p c t i", i=4),
            )

        def quantise(piece):
            c0, c, largest, slope, y, y_bf = piece
            y_codes = keep.tile([P, c], U32, name="y_codes%d" % c0, align_bytes=64)
            nc.vector.quantize_mx(
                out=y_codes[:].bitcast(FP8X4),
                scales=y_plane[:, c0 : c0 + c],
                in_=y_bf[:].rearrange("p c t -> p (c t)"),
            )
            nc.sync.dma_start(out_words[:, c0 : c0 + c], y_codes[:].bitcast(I32))

        waiting = None
        for c0, c in starts(PIECES_2):
            work = ring2.tile([P, PACK * c * (MEMBERS + 1)], F32, name="work", tag="work")
            members = work[:, : PACK * c * MEMBERS].rearrange("p (t c m) -> p t c m", t=PACK, m=MEMBERS)
            smallest = work[:, PACK * c * MEMBERS :]
            for t in range(PACK):
                fetch(members[:, t], h2_rows[t], n2_t, c0, c)
            pairs = members.rearrange("p t c m -> p (t c) m")
            low2 = ring.tile([P, PACK * c, 2], F32, name="low2", tag="low2")
            high2 = ring.tile([P, PACK * c, 2], F32, name="high2", tag="high2")
            rise = ring.tile([P, PACK, c], F32, name="rise", tag="rise")
            largest = ring.tile([P, PACK, c], F32, name="largest2", tag="largest2")
            slope = ring.tile([P, PACK, c], F32, name="slope", tag="slope")
            y = keep.tile([P, PACK, c], F32, name="y%d" % c0)
            y_bf = keep.tile([P, c, PACK], BF16, name="y_bf%d" % c0, align_bytes=64)
            for part in (slice(0, 2 * c), slice(2 * c, 4 * c)):
                nc.vector.tensor_tensor(low2[:, part], pairs[:, part, 0:2], pairs[:, part, 2:4], ALU.min)
                nc.vector.tensor_tensor(high2[:, part], pairs[:, part, 0:2], pairs[:, part, 2:4], ALU.max)
            nc.vector.tensor_tensor(smallest, low2[:, :, 0], low2[:, :, 1], ALU.min)
            if waiting is not None:
                product(waiting)
            nc.vector.tensor_tensor(
                rise[:], h2_all[:, :, c0 : c0 + c], smallest.rearrange("p (t c) -> p t c", t=PACK), ALU.subtract
            )
            nc.scalar.activation(slope[:], rise[:], ACT.Tanh)
            if waiting is not None:
                round_y(waiting)
            nc.vector.tensor_tensor(largest[:].rearrange("p t c -> p (t c)"), high2[:, :, 0], high2[:, :, 1], ALU.max)
            if waiting is not None:
                quantise(waiting)
            waiting = (c0, c, largest, slope, y, y_bf)
        nc.vector.tensor_tensor(
            y_bf[:], largest[:].rearrange("p t c -> p c t"), slope[:].rearrange("p t c -> p c t"), ALU.mult
        )
        product(waiting)
        quantise(waiting)

        for q in range(4):
            queue = nc.sync if q % 2 == 0 else nc.scalar
            queue.dma_start(out_2[0, 4 * q : 4 * q + 4, :].bitcast(I32), y_plane[32 * q : 32 * q + 4, :].bitcast(I32))
